import numpy as np
import ml_dtypes


def mxq(x, axis, fmt="e4m3"):
    dtype, down = {"e4m3": (ml_dtypes.float8_e4m3fn, 7), "e5m2": (ml_dtypes.float8_e5m2, 14)}[fmt]
    v = np.moveaxis(np.asarray(x, np.float32).astype(ml_dtypes.bfloat16).astype(np.float64), axis, -1)
    blocks = v.reshape(v.shape[:-1] + (-1, 32))
    amax = np.abs(blocks).max(-1, keepdims=True)
    byte = np.maximum(np.where(amax > 0, np.frexp(amax)[1] - 1 + 127, 0) - down, 1)
    scale = np.exp2(byte - 127.0)
    codes = (blocks / scale).astype(np.float32).astype(dtype).astype(np.float64)
    return np.moveaxis((codes * scale).reshape(v.shape), -1, axis)


WIDE = False


def mx_kscale(k, group=512):
    if not WIDE:
        return np.ones(k)
    levels = np.array([18, -18])
    if group != 512:
        return np.exp2(np.random.permutation(np.resize(levels, k // group))).repeat(group)
    if k % 512:
        return np.exp2(np.random.permutation(np.resize(levels, k // 32))).repeat(32)
    a = np.empty((k // 512, 16))
    for p in range(k // 512):
        a[p, :8] = np.random.permutation(np.resize(levels, 8))
        for g in range(8):
            far = levels[np.abs(levels - a[p, g]) >= 10]
            a[p, g + 8] = far[np.random.randint(len(far))]
    return np.exp2(a.ravel()).repeat(32)


def f64(x):
    return np.asarray(x).astype(np.float64)


G, D, M, O, N = 4, 128, 128, 128, 512


def setup_inputs():
    n = np.random.standard_normal
    s_d = mx_kscale(D, 0)
    s_o = mx_kscale(O, 0)
    return {
        "x": (n((G, D, N)) * s_d[:, None]).astype(np.float32),
        "w1": (n((G, D, M)) / np.sqrt(D) / s_d[:, None]).astype(np.float32),
        "w2": (n((G, D, M)) / np.sqrt(D) / s_d[:, None]).astype(np.float32),
        "tp": (np.random.uniform(0.5, 1.2, (G, M, 1))).astype(np.float32),
        "wo": (n((G, O, M)) / np.sqrt(O) / s_o[:, None]).astype(np.float32),
        "dy": (n((G, O, N)) * s_o[:, None]).astype(np.float32),
        "old": (0.3 * n((G, M, N))).astype(np.float32),
    }


def reference(x, w1, w2, tp, wo, dy, old):
    w1q = mxq(f64(w1), 1, "e4m3")
    xq = mxq(f64(x), 1, "e4m3")
    z1 = w1q.transpose(0, 2, 1) @ xq
    w2q = mxq(f64(w2), 1, "e4m3")
    z2 = w2q.transpose(0, 2, 1) @ xq
    p1 = np.exp(z1 * f64(tp) - np.max(z1 * f64(tp), axis=-1, keepdims=True))
    zs = np.sum(p1, axis=-1, keepdims=True)
    woq = mxq(f64(wo), 1, "e4m3")
    dyq = mxq(f64(dy), 1, "e4m3")
    c0 = woq.transpose(0, 2, 1) @ dyq
    dzs = np.sum(c0 * 512.0 * z2 * p1 / np.square(zs) * (-1.0), axis=-1, keepdims=True)
    dp1 = c0 * 512.0 * z2 / zs + dzs
    dz1 = dp1 * p1 * f64(tp)
    y = dz1 + f64(old)
    return y

@@ -1,0 +1,190 @@
+from contextlib import ExitStack
+
+import concourse.mybir as mybir
+
+G, D, M, N = 4, 128, 128, 512
+FLOPS = 3 * 2 * G * D * M * N
+
+F32 = mybir.dt.float32
+BF16 = mybir.dt.bfloat16
+U32 = mybir.dt.uint32
+U8 = mybir.dt.uint8
+FP8X4 = mybir.dt.float8_e4m3fn_x4
+ALU = mybir.AluOpType
+ACT = mybir.ActivationFunctionType
+
+P = 128
+PACK = 4
+ROWS = D // PACK
+RUN = 4
+GAIN = 512.0
+
+
+def tile_rows_browsoft_kernel(tc, x, w1, w2, tp, wo, dy, old, out):
+    nc = tc.nc
+    with ExitStack() as ctx:
+        sb = ctx.enter_context(tc.tile_pool(name="sb", bufs=1))
+        ps = ctx.enter_context(tc.psum_pool(name="ps", bufs=1))
+        ctx.enter_context(tc.manual_schedule())
+
+        def load(name, src, width):
+            raw = sb.tile([P, PACK, width], F32, name=name)
+            nc.sync.dma_start(out=raw[:], in_=src.rearrange("g (p j) c -> (g p) j c", j=PACK))
+            return raw
+
+        def operand(name, width):
+            packed = sb.tile([P, width, PACK], BF16, name=name + "_bf16", align_bytes=64)
+            codes = sb.tile([P, width], U32, name=name + "_codes", align_bytes=64)
+            scales = sb.tile([P, width], U8, name=name + "_scales", align_bytes=64)
+            return packed, codes, scales
+
+        def interleave(copy, op, at, raw, c0, c1):
+            dst = op[0][:, at + c0 : at + c1, :].rearrange("p (c i) j -> p c j i", i=RUN)
+            src = raw[:, :, c0:c1].rearrange("p j (c i) -> p c j i", i=RUN)
+            copy(out=dst, in_=src)
+
+        def quantize(op, c0, c1):
+            nc.vector.quantize_mx(
+                out=op[1][:, c0:c1].bitcast(FP8X4),
+                scales=op[2][:, c0:c1],
+                in_=op[0][:, c0:c1, :].rearrange("p c j -> p (c j)"),
+            )
+
+        def product(bank, g, wq, at, aq):
+            rows = slice(ROWS * g, ROWS * (g + 1))
+            nc.tensor.matmul_mx(
+                out=bank[:],
+                lhsT=wq[1][rows, at : at + M].bitcast(FP8X4),
+                lhsT_scale=wq[2][rows, at : at + M],
+                rhs=aq[1][rows, :].bitcast(FP8X4),
+                rhs_scale=aq[2][rows, :],
+                start=True,
+                stop=True,
+            )
+
+        tp_rows = sb.tile([P, P], F32, name="tp_rows", align_bytes=64)
+        tp_cols = sb.tile([P, P], F32, name="tp_cols", align_bytes=64)
+        nc.vector.memset(tp_rows[:], 0.0)
+        nc.scalar.dma_start(
+            out=tp_rows[0:P:32, :].rearrange("a (g c) -> a g c", g=G),
+            in_=tp.rearrange("g (a c) o -> a g (c o)", c=32),
+        )
+
+        x_raw = load("x_raw", x, N)
+        w1_raw = load("w1_raw", w1, M)
+        w2_raw = load("w2_raw", w2, M)
+        wo_raw = load("wo_raw", wo, M)
+        dy_raw = load("dy_raw", dy, N)
+        old_sb = []
+        for h in range(2):
+            t = sb.tile([P, 2, N], F32, name="old_%d" % h)
+            nc.sync.dma_start(out=t[:], in_=old[2 * h : 2 * h + 2].rearrange("g m n -> m g n"))
+            old_sb.extend([t[:, 0, :], t[:, 1, :]])
+
+        neg_tp = sb.tile([P, G], F32, name="neg_tp")
+        neg_gain = sb.tile([P, G], F32, name="neg_gain")
+        nc.vector.transpose(out=tp_cols[:], in_=tp_rows[:])
+        nc.vector.tensor_scalar(out=neg_tp[:], in0=tp_cols[:, 0:P:32], scalar1=-1.0, scalar2=None, op0=ALU.mult)
+        nc.vector.tensor_scalar(out=neg_gain[:], in0=tp_cols[:, 0:P:32], scalar1=-GAIN, scalar2=None, op0=ALU.mult)
+
+        xq = operand("x", N)
+        dq = operand("dy", N)
+        w1q = operand("w1", M)
+        wbq = operand("w2wo", 2 * M)
+        bank_a = [ps.tile([M, N], F32, name="bank_a%d" % g) for g in range(G)]
+        bank_b = [ps.tile([M, N], F32, name="bank_b%d" % g) for g in range(G)]
+
+        neg_s = [sb.tile([M, N], F32, name="neg_s%d" % g) for g in range(G)]
+        p1 = [sb.tile([M, N], F32, name="p1_%d" % g) for g in range(G)]
+        pz = [sb.tile([M, N], F32, name="pz%d" % g) for g in range(G)]
+        neg_u = [sb.tile([M, N], F32, name="neg_u%d" % g) for g in range(G)]
+        part = [sb.tile([M, N], F32, name="part%d" % g) for g in range(G)]
+        res = [sb.tile([M, N], F32, name="res%d" % g) for g in range(G)]
+        neg_max = sb.tile([M, G], F32, name="neg_max")
+        zs = sb.tile([M, G], F32, name="zs")
+        inv_zs = sb.tile([M, G], F32, name="inv_zs")
+        neg_sum = sb.tile([M, G], F32, name="neg_sum")
+        shift = sb.tile([M, G], F32, name="shift")
+
+        def col(t, g):
+            return t[:, g : g + 1]
+
+        def scores(g):
+            nc.vector.tensor_scalar(
+                out=neg_s[g][:], in0=bank_a[g][:], scalar1=col(neg_tp, g), scalar2=None,
+                op0=ALU.mult, op1=ALU.min, accum_out=col(neg_max, g),
+            )
+
+        def weights(g):
+            nc.scalar.activation(
+                out=p1[g][:], in_=neg_s[g][:], func=ACT.Exp, scale=-1.0, bias=col(neg_max, g), accum_out=col(zs, g),
+            )
+
+        def times_z2(g):
+            nc.vector.scalar_tensor_tensor(
+                out=pz[g][:], in0=bank_b[g][:], scalar=col(neg_gain, g), in1=p1[g][:], op0=ALU.mult, op1=ALU.mult,
+            )
+
+        def times_c0(g):
+            nc.vector.scalar_tensor_tensor(
+                out=neg_u[g][:], in0=bank_a[g][:], scalar=col(inv_zs, g), in1=pz[g][:],
+                op0=ALU.mult, op1=ALU.mult, accum_out=col(neg_sum, g),
+            )
+            nc.scalar.activation(out=col(shift, g), in_=col(neg_sum, g), func=ACT.Copy, scale=col(inv_zs, g))
+
+        def add_old(g):
+            nc.vector.tensor_tensor(out=part[g][:], in0=old_sb[g], in1=neg_u[g][:], op=ALU.subtract)
+
+        def finish(g):
+            nc.vector.scalar_tensor_tensor(
+                out=res[g][:], in0=p1[g][:], scalar=col(shift, g), in1=part[g][:], op0=ALU.mult, op1=ALU.add,
+            )
+            nc.sync.dma_start(out=out[g], in_=res[g][:])
+
+        H = N // 2
+        interleave(nc.vector.tensor_copy, xq, 0, x_raw, 0, H)
+        interleave(nc.scalar.copy, xq, 0, x_raw, H, N)
+        interleave(nc.vector.tensor_copy, w1q, 0, w1_raw, 0, M)
+        quantize(xq, 0, H)
+        quantize(w1q, 0, M)
+        quantize(xq, H, N)
+        for g in range(G):
+            product(bank_a[g], g, w1q, 0, xq)
+        interleave(nc.scalar.copy, wbq, 0, w2_raw, 0, M)
+        interleave(nc.vector.tensor_copy, wbq, M, wo_raw, 0, M)
+        scores(0)
+        quantize(wbq, 0, 2 * M)
+        for g in range(G):
+            product(bank_b[g], g, wbq, 0, xq)
+        weights(0)
+        scores(1)
+        interleave(nc.scalar.copy, dq, 0, dy_raw, 0, H)
+        weights(1)
+        scores(2)
+        scores(3)
+        interleave(nc.scalar.copy, dq, 0, dy_raw, H, H + H // 2)
+        weights(2)
+        weights(3)
+        interleave(nc.vector.tensor_copy, dq, 0, dy_raw, H + H // 2, N)
+        quantize(dq, 0, H)
+        times_z2(0)
+        quantize(dq, H, N)
+        for g in range(G):
+            product(bank_a[g], g, wbq, M, dq)
+        times_z2(1)
+        nc.vector.reciprocal(out=inv_zs[:, 0:2], in_=zs[:, 0:2])
+        times_z2(2)
+        times_c0(0)
+        nc.vector.reciprocal(out=inv_zs[:, 2:4], in_=zs[:, 2:4])
+        times_c0(1)
+        add_old(0)
+        times_z2(3)
+        finish(0)
+        times_c0(2)
+        add_old(1)
+        times_c0(3)
+        finish(1)
+        add_old(2)
+        add_old(3)
+        finish(2)
+        finish(3)

@@ -16,7 +16,7 @@ ACT = mybir.ActivationFunctionType
 P = 128
 PACK = 4
 ROWS = D // PACK
-RUN = 4
+RUN = 2
 GAIN = 512.0
 
 
@@ -38,9 +38,9 @@ def tile_rows_browsoft_kernel(tc, x, w1, w2, tp, wo, dy, old, out):
             scales = sb.tile([P, width], U8, name=name + "_scales", align_bytes=64)
             return packed, codes, scales
 
-        def interleave(copy, op, at, raw, c0, c1):
-            dst = op[0][:, at + c0 : at + c1, :].rearrange("p (c i) j -> p c j i", i=RUN)
-            src = raw[:, :, c0:c1].rearrange("p j (c i) -> p c j i", i=RUN)
+        def interleave(copy, op, at, raw, c0, c1, run=RUN):
+            dst = op[0][:, at + c0 : at + c1, :].rearrange("p (c i) j -> p c j i", i=run)
+            src = raw[:, :, c0:c1].rearrange("p j (c i) -> p c j i", i=run)
             copy(out=dst, in_=src)
 
         def quantize(op, c0, c1):
@@ -83,9 +83,11 @@ def tile_rows_browsoft_kernel(tc, x, w1, w2, tp, wo, dy, old, out):
 
         neg_tp = sb.tile([P, G], F32, name="neg_tp")
         neg_gain = sb.tile([P, G], F32, name="neg_gain")
-        nc.vector.transpose(out=tp_cols[:], in_=tp_rows[:])
-        nc.vector.tensor_scalar(out=neg_tp[:], in0=tp_cols[:, 0:P:32], scalar1=-1.0, scalar2=None, op0=ALU.mult)
-        nc.vector.tensor_scalar(out=neg_gain[:], in0=tp_cols[:, 0:P:32], scalar1=-GAIN, scalar2=None, op0=ALU.mult)
+
+        def tempers():
+            nc.vector.transpose(out=tp_cols[:], in_=tp_rows[:])
+            nc.vector.tensor_scalar(out=neg_tp[:], in0=tp_cols[:, 0:P:32], scalar1=-1.0, scalar2=None, op0=ALU.mult)
+            nc.vector.tensor_scalar(out=neg_gain[:], in0=tp_cols[:, 0:P:32], scalar1=-GAIN, scalar2=None, op0=ALU.mult)
 
         xq = operand("x", N)
         dq = operand("dy", N)
@@ -98,7 +100,8 @@ def tile_rows_browsoft_kernel(tc, x, w1, w2, tp, wo, dy, old, out):
         p1 = [sb.tile([M, N], F32, name="p1_%d" % g) for g in range(G)]
         pz = [sb.tile([M, N], F32, name="pz%d" % g) for g in range(G)]
         neg_u = [sb.tile([M, N], F32, name="neg_u%d" % g) for g in range(G)]
-        part = [sb.tile([M, N], F32, name="part%d" % g) for g in range(G)]
+        part01 = sb.tile([M, N], F32, name="part01")
+        part = [part01, part01] + [sb.tile([M, N], F32, name="part%d" % g) for g in range(2, G)]
         res = [sb.tile([M, N], F32, name="res%d" % g) for g in range(G)]
         neg_max = sb.tile([M, G], F32, name="neg_max")
         zs = sb.tile([M, G], F32, name="zs")
@@ -132,59 +135,64 @@ def tile_rows_browsoft_kernel(tc, x, w1, w2, tp, wo, dy, old, out):
             )
             nc.scalar.activation(out=col(shift, g), in_=col(neg_sum, g), func=ACT.Copy, scale=col(inv_zs, g))
 
-        def add_old(g):
-            nc.vector.tensor_tensor(out=part[g][:], in0=old_sb[g], in1=neg_u[g][:], op=ALU.subtract)
+        def pool_copy(out, in_):
+            nc.gpsimd.tensor_scalar(out=out, in0=in_, scalar1=1.0, scalar2=0.0, op0=ALU.mult, op1=ALU.add)
 
-        def finish(g):
+        def add_old(g, engine, cols=slice(0, N)):
+            engine.tensor_tensor(out=part[g][:, cols], in0=old_sb[g][:, cols], in1=neg_u[g][:, cols], op=ALU.subtract)
+
+        def finish(g, cols=slice(0, N)):
             nc.vector.scalar_tensor_tensor(
-                out=res[g][:], in0=p1[g][:], scalar=col(shift, g), in1=part[g][:], op0=ALU.mult, op1=ALU.add,
+                out=res[g][:, cols], in0=p1[g][:, cols], scalar=col(shift, g), in1=part[g][:, cols], op0=ALU.mult, op1=ALU.add,
             )
-            nc.sync.dma_start(out=out[g], in_=res[g][:])
+            nc.sync.dma_start(out=out[g, :, cols], in_=res[g][:, cols])
 
         H = N // 2
-        interleave(nc.vector.tensor_copy, xq, 0, x_raw, 0, H)
-        interleave(nc.scalar.copy, xq, 0, x_raw, H, N)
-        interleave(nc.vector.tensor_copy, w1q, 0, w1_raw, 0, M)
+        V, S = nc.vector.tensor_copy, nc.scalar.copy
+        interleave(V, xq, 0, x_raw, 0, H)
+        interleave(S, xq, 0, x_raw, H, N)
+        interleave(V, w1q, 0, w1_raw, 0, M)
         quantize(xq, 0, H)
         quantize(w1q, 0, M)
         quantize(xq, H, N)
         for g in range(G):
             product(bank_a[g], g, w1q, 0, xq)
-        interleave(nc.scalar.copy, wbq, 0, w2_raw, 0, M)
-        interleave(nc.vector.tensor_copy, wbq, M, wo_raw, 0, M)
+        interleave(S, wbq, 0, w2_raw, 0, M)
+        interleave(S, wbq, M, wo_raw, 0, M)
+        tempers()
         scores(0)
         quantize(wbq, 0, 2 * M)
         for g in range(G):
             product(bank_b[g], g, wbq, 0, xq)
         weights(0)
         scores(1)
-        interleave(nc.scalar.copy, dq, 0, dy_raw, 0, H)
+        interleave(S, dq, 0, dy_raw, 0, H)
+        interleave(pool_copy, dq, 0, dy_raw, H, N, 1)
         weights(1)
         scores(2)
-        scores(3)
-        interleave(nc.scalar.copy, dq, 0, dy_raw, H, H + H // 2)
-        weights(2)
-        weights(3)
-        interleave(nc.vector.tensor_copy, dq, 0, dy_raw, H + H // 2, N)
-        quantize(dq, 0, H)
         times_z2(0)
-        quantize(dq, H, N)
+        scores(3)
+        quantize(dq, 0, N)
         for g in range(G):
             product(bank_a[g], g, wbq, M, dq)
+        weights(2)
+        weights(3)
         times_z2(1)
         nc.vector.reciprocal(out=inv_zs[:, 0:2], in_=zs[:, 0:2])
         times_z2(2)
         times_c0(0)
+        add_old(0, nc.gpsimd)
         nc.vector.reciprocal(out=inv_zs[:, 2:4], in_=zs[:, 2:4])
         times_c0(1)
-        add_old(0)
-        times_z2(3)
-        finish(0)
         times_c0(2)
-        add_old(1)
+        finish(0)
+        add_old(1, nc.gpsimd)
+        times_z2(3)
         times_c0(3)
+        add_old(2, nc.vector)
         finish(1)
-        add_old(2)
-        add_old(3)
         finish(2)
-        finish(3)
+        add_old(3, nc.vector, slice(0, H))
+        add_old(3, nc.vector, slice(H, N))
+        finish(3, slice(0, H))
+        finish(3, slice(H, N))

@@ -65,12 +65,12 @@ def tile_rows_browsoft_kernel(tc, x, w1, w2, tp, wo, dy, old, out):
         tp_rows = sb.tile([P, P], F32, name="tp_rows", align_bytes=64)
         tp_cols = sb.tile([P, P], F32, name="tp_cols", align_bytes=64)
         nc.vector.memset(tp_rows[:], 0.0)
-        nc.scalar.dma_start(
+
+        x_raw = load("x_raw", x, N)
+        nc.sync.dma_start(
             out=tp_rows[0:P:32, :].rearrange("a (g c) -> a g c", g=G),
             in_=tp.rearrange("g (a c) o -> a g (c o)", c=32),
         )
-
-        x_raw = load("x_raw", x, N)
         w1_raw = load("w1_raw", w1, M)
         w2_raw = load("w2_raw", w2, M)
         wo_raw = load("wo_raw", wo, M)
@@ -100,14 +100,15 @@ def tile_rows_browsoft_kernel(tc, x, w1, w2, tp, wo, dy, old, out):
         p1 = [sb.tile([M, N], F32, name="p1_%d" % g) for g in range(G)]
         pz = [sb.tile([M, N], F32, name="pz%d" % g) for g in range(G)]
         neg_u = [sb.tile([M, N], F32, name="neg_u%d" % g) for g in range(G)]
-        part01 = sb.tile([M, N], F32, name="part01")
-        part = [part01, part01] + [sb.tile([M, N], F32, name="part%d" % g) for g in range(2, G)]
+        part = [sb.tile([M, N], F32, name="part%d" % g) for g in range(G)]
         res = [sb.tile([M, N], F32, name="res%d" % g) for g in range(G)]
         neg_max = sb.tile([M, G], F32, name="neg_max")
         zs = sb.tile([M, G], F32, name="zs")
         inv_zs = sb.tile([M, G], F32, name="inv_zs")
         neg_sum = sb.tile([M, G], F32, name="neg_sum")
         shift = sb.tile([M, G], F32, name="shift")
+
+        z2s = {}
 
         def col(t, g):
             return t[:, g : g + 1]
@@ -127,6 +128,13 @@ def tile_rows_browsoft_kernel(tc, x, w1, w2, tp, wo, dy, old, out):
             nc.vector.scalar_tensor_tensor(
                 out=pz[g][:], in0=bank_b[g][:], scalar=col(neg_gain, g), in1=p1[g][:], op0=ALU.mult, op1=ALU.mult,
             )
+
+        def z2_out(g):
+            z2s[g] = sb.tile([M, N], F32, name="z2s%d" % g)
+            nc.scalar.activation(out=z2s[g][:], in_=bank_b[g][:], func=ACT.Copy, scale=col(neg_gain, g))
+
+        def times_z2_pool(g):
+            nc.gpsimd.tensor_tensor(out=pz[g][:], in0=z2s[g][:], in1=p1[g][:], op=ALU.mult)
 
         def times_c0(g):
             nc.vector.scalar_tensor_tensor(
@@ -155,40 +163,46 @@ def tile_rows_browsoft_kernel(tc, x, w1, w2, tp, wo, dy, old, out):
         quantize(xq, 0, H)
         quantize(w1q, 0, M)
         quantize(xq, H, N)
-        for g in range(G):
+        for g in range(3):
             product(bank_a[g], g, w1q, 0, xq)
         interleave(S, wbq, 0, w2_raw, 0, M)
         interleave(S, wbq, M, wo_raw, 0, M)
         tempers()
-        scores(0)
         quantize(wbq, 0, 2 * M)
-        for g in range(G):
-            product(bank_b[g], g, wbq, 0, xq)
+        product(bank_b[0], 0, wbq, 0, xq)
+        product(bank_b[1], 1, wbq, 0, xq)
+        product(bank_a[3], 3, w1q, 0, xq)
+        product(bank_b[2], 2, wbq, 0, xq)
+        scores(0)
         weights(0)
         scores(1)
         interleave(S, dq, 0, dy_raw, 0, H)
         interleave(pool_copy, dq, 0, dy_raw, H, N, 1)
         weights(1)
+        z2_out(1)
         scores(2)
         times_z2(0)
-        scores(3)
         quantize(dq, 0, N)
-        for g in range(G):
-            product(bank_a[g], g, wbq, M, dq)
+        times_z2_pool(1)
+        product(bank_a[0], 0, wbq, M, dq)
+        product(bank_a[1], 1, wbq, M, dq)
+        product(bank_a[2], 2, wbq, M, dq)
+        product(bank_b[3], 3, wbq, 0, xq)
+        nc.vector.reciprocal(out=inv_zs[:, 0:2], in_=zs[:, 0:2])
+        scores(3)
+        product(bank_a[3], 3, wbq, M, dq)
         weights(2)
         weights(3)
-        times_z2(1)
-        nc.vector.reciprocal(out=inv_zs[:, 0:2], in_=zs[:, 0:2])
-        times_z2(2)
         times_c0(0)
         add_old(0, nc.gpsimd)
-        nc.vector.reciprocal(out=inv_zs[:, 2:4], in_=zs[:, 2:4])
+        times_z2(2)
         times_c0(1)
-        times_c0(2)
-        finish(0)
         add_old(1, nc.gpsimd)
+        nc.vector.reciprocal(out=inv_zs[:, 2:4], in_=zs[:, 2:4])
         times_z2(3)
+        times_c0(2)
         times_c0(3)
+        finish(0)
         add_old(2, nc.vector)
         finish(1)
         finish(2)

@@ -16,8 +16,11 @@ ACT = mybir.ActivationFunctionType
 P = 128
 PACK = 4
 ROWS = D // PACK
-RUN = 2
+SQUARE = 32
 GAIN = 512.0
+HALF = N // 2
+PAIR = 2
+DY_SCALAR = 304
 
 
 def tile_rows_browsoft_kernel(tc, x, w1, w2, tp, wo, dy, old, out):
@@ -33,31 +36,35 @@ def tile_rows_browsoft_kernel(tc, x, w1, w2, tp, wo, dy, old, out):
             return raw
 
         def operand(name, width):
-            packed = sb.tile([P, width, PACK], BF16, name=name + "_bf16", align_bytes=64)
-            codes = sb.tile([P, width], U32, name=name + "_codes", align_bytes=64)
-            scales = sb.tile([P, width], U8, name=name + "_scales", align_bytes=64)
-            return packed, codes, scales
+            return {
+                "values": sb.tile([P, width, PACK], BF16, name=name + "_bf16", align_bytes=64),
+                "codes": sb.tile([P, width], U32, name=name + "_codes", align_bytes=64),
+                "scales": sb.tile([P, width], U8, name=name + "_scales", align_bytes=64),
+            }
 
-        def interleave(copy, op, at, raw, c0, c1, run=RUN):
-            dst = op[0][:, at + c0 : at + c1, :].rearrange("p (c i) j -> p c j i", i=run)
-            src = raw[:, :, c0:c1].rearrange("p j (c i) -> p c j i", i=run)
+        def interleave(copy, mx, at, raw, first, last, run):
+            dst = mx["values"][:, at + first : at + last, :].rearrange("p (c i) j -> p c j i", i=run)
+            src = raw[:, :, first:last].rearrange("p j (c i) -> p c j i", i=run)
             copy(out=dst, in_=src)
 
-        def quantize(op, c0, c1):
+        def gpsimd_copy(out, in_):
+            nc.gpsimd.tensor_scalar(out=out, in0=in_, scalar1=1.0, scalar2=0.0, op0=ALU.mult, op1=ALU.add)
+
+        def quantize(mx, first, last):
             nc.vector.quantize_mx(
-                out=op[1][:, c0:c1].bitcast(FP8X4),
-                scales=op[2][:, c0:c1],
-                in_=op[0][:, c0:c1, :].rearrange("p c j -> p (c j)"),
+                out=mx["codes"][:, first:last].bitcast(FP8X4),
+                scales=mx["scales"][:, first:last],
+                in_=mx["values"][:, first:last, :].rearrange("p c j -> p (c j)"),
             )
 
-        def product(bank, g, wq, at, aq):
+        def product(bank, g, w_mx, at, act_mx):
             rows = slice(ROWS * g, ROWS * (g + 1))
             nc.tensor.matmul_mx(
                 out=bank[:],
-                lhsT=wq[1][rows, at : at + M].bitcast(FP8X4),
-                lhsT_scale=wq[2][rows, at : at + M],
-                rhs=aq[1][rows, :].bitcast(FP8X4),
-                rhs_scale=aq[2][rows, :],
+                lhsT=w_mx["codes"][rows, at : at + M].bitcast(FP8X4),
+                lhsT_scale=w_mx["scales"][rows, at : at + M],
+                rhs=act_mx["codes"][rows, :].bitcast(FP8X4),
+                rhs_scale=act_mx["scales"][rows, :],
                 start=True,
                 stop=True,
             )
@@ -68,39 +75,34 @@ def tile_rows_browsoft_kernel(tc, x, w1, w2, tp, wo, dy, old, out):
 
         x_raw = load("x_raw", x, N)
         nc.sync.dma_start(
-            out=tp_rows[0:P:32, :].rearrange("a (g c) -> a g c", g=G),
-            in_=tp.rearrange("g (a c) o -> a g (c o)", c=32),
+            out=tp_rows[0:P:SQUARE, :].rearrange("a (g c) -> a g c", g=G),
+            in_=tp.rearrange("g (a c) o -> a g (c o)", c=SQUARE),
         )
         w1_raw = load("w1_raw", w1, M)
         w2_raw = load("w2_raw", w2, M)
         wo_raw = load("wo_raw", wo, M)
         dy_raw = load("dy_raw", dy, N)
         old_sb = []
-        for h in range(2):
-            t = sb.tile([P, 2, N], F32, name="old_%d" % h)
-            nc.sync.dma_start(out=t[:], in_=old[2 * h : 2 * h + 2].rearrange("g m n -> m g n"))
-            old_sb.extend([t[:, 0, :], t[:, 1, :]])
+        for pair in range(G // 2):
+            old_pair = sb.tile([P, 2, N], F32, name="old_%d" % pair)
+            nc.sync.dma_start(out=old_pair[:], in_=old[2 * pair : 2 * pair + 2].rearrange("g m n -> m g n"))
+            old_sb.extend([old_pair[:, 0, :], old_pair[:, 1, :]])
 
         neg_tp = sb.tile([P, G], F32, name="neg_tp")
         neg_gain = sb.tile([P, G], F32, name="neg_gain")
 
-        def tempers():
-            nc.vector.transpose(out=tp_cols[:], in_=tp_rows[:])
-            nc.vector.tensor_scalar(out=neg_tp[:], in0=tp_cols[:, 0:P:32], scalar1=-1.0, scalar2=None, op0=ALU.mult)
-            nc.vector.tensor_scalar(out=neg_gain[:], in0=tp_cols[:, 0:P:32], scalar1=-GAIN, scalar2=None, op0=ALU.mult)
-
-        xq = operand("x", N)
-        dq = operand("dy", N)
-        w1q = operand("w1", M)
-        wbq = operand("w2wo", 2 * M)
-        bank_a = [ps.tile([M, N], F32, name="bank_a%d" % g) for g in range(G)]
-        bank_b = [ps.tile([M, N], F32, name="bank_b%d" % g) for g in range(G)]
+        x_mx = operand("x", N)
+        dy_mx = operand("dy", N)
+        w1_mx = operand("w1", M)
+        w2wo_mx = operand("w2wo", 2 * M)
+        bank_z1c0 = [ps.tile([M, N], F32, name="bank_z1c0_%d" % g) for g in range(G)]
+        bank_z2 = [ps.tile([M, N], F32, name="bank_z2_%d" % g) for g in range(G)]
 
         neg_s = [sb.tile([M, N], F32, name="neg_s%d" % g) for g in range(G)]
         p1 = [sb.tile([M, N], F32, name="p1_%d" % g) for g in range(G)]
-        pz = [sb.tile([M, N], F32, name="pz%d" % g) for g in range(G)]
+        neg_pz = [sb.tile([M, N], F32, name="neg_pz%d" % g) for g in range(G)]
         neg_u = [sb.tile([M, N], F32, name="neg_u%d" % g) for g in range(G)]
-        part = [sb.tile([M, N], F32, name="part%d" % g) for g in range(G)]
+        old_u = [sb.tile([M, N], F32, name="old_u%d" % g) for g in range(G)]
         res = [sb.tile([M, N], F32, name="res%d" % g) for g in range(G)]
         neg_max = sb.tile([M, G], F32, name="neg_max")
         zs = sb.tile([M, G], F32, name="zs")
@@ -108,105 +110,102 @@ def tile_rows_browsoft_kernel(tc, x, w1, w2, tp, wo, dy, old, out):
         neg_sum = sb.tile([M, G], F32, name="neg_sum")
         shift = sb.tile([M, G], F32, name="shift")
 
-        z2s = {}
-
-        def col(t, g):
-            return t[:, g : g + 1]
+        def col(stats, g):
+            return stats[:, g : g + 1]
 
         def scores(g):
             nc.vector.tensor_scalar(
-                out=neg_s[g][:], in0=bank_a[g][:], scalar1=col(neg_tp, g), scalar2=None,
+                out=neg_s[g][:], in0=bank_z1c0[g][:], scalar1=col(neg_tp, g), scalar2=None,
                 op0=ALU.mult, op1=ALU.min, accum_out=col(neg_max, g),
             )
 
-        def weights(g):
+        def exps(g):
             nc.scalar.activation(
                 out=p1[g][:], in_=neg_s[g][:], func=ACT.Exp, scale=-1.0, bias=col(neg_max, g), accum_out=col(zs, g),
             )
 
         def times_z2(g):
             nc.vector.scalar_tensor_tensor(
-                out=pz[g][:], in0=bank_b[g][:], scalar=col(neg_gain, g), in1=p1[g][:], op0=ALU.mult, op1=ALU.mult,
+                out=neg_pz[g][:], in0=bank_z2[g][:], scalar=col(neg_gain, g), in1=p1[g][:], op0=ALU.mult, op1=ALU.mult,
             )
 
-        def z2_out(g):
-            z2s[g] = sb.tile([M, N], F32, name="z2s%d" % g)
-            nc.scalar.activation(out=z2s[g][:], in_=bank_b[g][:], func=ACT.Copy, scale=col(neg_gain, g))
+        def times_z2_off_vector(g):
+            neg_z2 = sb.tile([M, N], F32, name="neg_z2")
+            nc.scalar.activation(out=neg_z2[:], in_=bank_z2[g][:], func=ACT.Copy, scale=col(neg_gain, g))
+            nc.gpsimd.tensor_tensor(out=neg_pz[g][:], in0=neg_z2[:], in1=p1[g][:], op=ALU.mult)
 
-        def times_z2_pool(g):
-            nc.gpsimd.tensor_tensor(out=pz[g][:], in0=z2s[g][:], in1=p1[g][:], op=ALU.mult)
+        def inverses(first, last):
+            nc.vector.reciprocal(out=inv_zs[:, first:last], in_=zs[:, first:last])
 
         def times_c0(g):
             nc.vector.scalar_tensor_tensor(
-                out=neg_u[g][:], in0=bank_a[g][:], scalar=col(inv_zs, g), in1=pz[g][:],
+                out=neg_u[g][:], in0=bank_z1c0[g][:], scalar=col(inv_zs, g), in1=neg_pz[g][:],
                 op0=ALU.mult, op1=ALU.mult, accum_out=col(neg_sum, g),
             )
             nc.scalar.activation(out=col(shift, g), in_=col(neg_sum, g), func=ACT.Copy, scale=col(inv_zs, g))
 
-        def pool_copy(out, in_):
-            nc.gpsimd.tensor_scalar(out=out, in0=in_, scalar1=1.0, scalar2=0.0, op0=ALU.mult, op1=ALU.add)
+        def add_old(engine, g, cols):
+            engine.tensor_tensor(out=old_u[g][:, cols], in0=old_sb[g][:, cols], in1=neg_u[g][:, cols], op=ALU.subtract)
 
-        def add_old(g, engine, cols=slice(0, N)):
-            engine.tensor_tensor(out=part[g][:, cols], in0=old_sb[g][:, cols], in1=neg_u[g][:, cols], op=ALU.subtract)
-
-        def finish(g, cols=slice(0, N)):
+        def finish(g, cols):
             nc.vector.scalar_tensor_tensor(
-                out=res[g][:, cols], in0=p1[g][:, cols], scalar=col(shift, g), in1=part[g][:, cols], op0=ALU.mult, op1=ALU.add,
+                out=res[g][:, cols], in0=p1[g][:, cols], scalar=col(shift, g), in1=old_u[g][:, cols],
+                op0=ALU.mult, op1=ALU.add,
             )
             nc.sync.dma_start(out=out[g, :, cols], in_=res[g][:, cols])
 
-        H = N // 2
-        V, S = nc.vector.tensor_copy, nc.scalar.copy
-        interleave(V, xq, 0, x_raw, 0, H)
-        interleave(S, xq, 0, x_raw, H, N)
-        interleave(V, w1q, 0, w1_raw, 0, M)
-        quantize(xq, 0, H)
-        quantize(w1q, 0, M)
-        quantize(xq, H, N)
-        for g in range(3):
-            product(bank_a[g], g, w1q, 0, xq)
-        interleave(S, wbq, 0, w2_raw, 0, M)
-        interleave(S, wbq, M, wo_raw, 0, M)
-        tempers()
-        quantize(wbq, 0, 2 * M)
-        product(bank_b[0], 0, wbq, 0, xq)
-        product(bank_b[1], 1, wbq, 0, xq)
-        product(bank_a[3], 3, w1q, 0, xq)
-        product(bank_b[2], 2, wbq, 0, xq)
-        scores(0)
-        weights(0)
-        scores(1)
-        interleave(S, dq, 0, dy_raw, 0, H)
-        interleave(pool_copy, dq, 0, dy_raw, H, N, 1)
-        weights(1)
-        z2_out(1)
-        scores(2)
+        whole = slice(0, N)
+        halves = [slice(0, HALF), slice(HALF, N)]
+
+        interleave(nc.vector.tensor_copy, x_mx, 0, x_raw, 0, HALF, PAIR)
+        interleave(nc.scalar.copy, x_mx, 0, x_raw, HALF, N, PAIR)
+        interleave(nc.vector.tensor_copy, w1_mx, 0, w1_raw, 0, M, PAIR)
+        quantize(x_mx, 0, HALF)
+        quantize(w1_mx, 0, M)
+        quantize(x_mx, HALF, N)
+        for g in range(G):
+            product(bank_z1c0[g], g, w1_mx, 0, x_mx)
+
+        interleave(nc.scalar.copy, w2wo_mx, 0, w2_raw, 0, M, PAIR)
+        interleave(nc.scalar.copy, w2wo_mx, M, wo_raw, 0, M, PAIR)
+        nc.vector.transpose(out=tp_cols[:], in_=tp_rows[:])
+        nc.vector.tensor_scalar(out=neg_tp[:], in0=tp_cols[:, 0:P:SQUARE], scalar1=-1.0, scalar2=None, op0=ALU.mult)
+        nc.vector.tensor_scalar(out=neg_gain[:], in0=tp_cols[:, 0:P:SQUARE], scalar1=-GAIN, scalar2=None, op0=ALU.mult)
+        quantize(w2wo_mx, 0, 2 * M)
+        for g in range(G):
+            product(bank_z2[g], g, w2wo_mx, 0, x_mx)
+
+        interleave(nc.scalar.copy, dy_mx, 0, dy_raw, 0, DY_SCALAR, PAIR)
+        interleave(gpsimd_copy, dy_mx, 0, dy_raw, DY_SCALAR, N, 1)
+        for g in range(G):
+            scores(g)
+        quantize(dy_mx, 0, N)
+        for g in range(G):
+            product(bank_z1c0[g], g, w2wo_mx, M, dy_mx)
+
+        exps(0)
+        exps(1)
         times_z2(0)
-        quantize(dq, 0, N)
-        times_z2_pool(1)
-        product(bank_a[0], 0, wbq, M, dq)
-        product(bank_a[1], 1, wbq, M, dq)
-        product(bank_a[2], 2, wbq, M, dq)
-        product(bank_b[3], 3, wbq, 0, xq)
-        nc.vector.reciprocal(out=inv_zs[:, 0:2], in_=zs[:, 0:2])
-        scores(3)
-        product(bank_a[3], 3, wbq, M, dq)
-        weights(2)
-        weights(3)
+        times_z2_off_vector(1)
+        exps(2)
+        exps(3)
+        inverses(0, 2)
+
         times_c0(0)
-        add_old(0, nc.gpsimd)
+        add_old(nc.gpsimd, 0, whole)
         times_z2(2)
         times_c0(1)
-        add_old(1, nc.gpsimd)
-        nc.vector.reciprocal(out=inv_zs[:, 2:4], in_=zs[:, 2:4])
+        add_old(nc.gpsimd, 1, whole)
+        inverses(2, 4)
         times_z2(3)
         times_c0(2)
         times_c0(3)
-        finish(0)
-        add_old(2, nc.vector)
-        finish(1)
-        finish(2)
-        add_old(3, nc.vector, slice(0, H))
-        add_old(3, nc.vector, slice(H, N))
-        finish(3, slice(0, H))
-        finish(3, slice(H, N))
+
+        finish(0, whole)
+        add_old(nc.vector, 2, whole)
+        finish(1, whole)
+        finish(2, whole)
+        for cols in halves:
+            add_old(nc.vector, 3, cols)
+        for cols in halves:
+            finish(3, cols)

from contextlib import ExitStack

import concourse.mybir as mybir

G, D, M, N = 4, 128, 128, 512
FLOPS = 3 * 2 * G * D * M * N

F32 = mybir.dt.float32
BF16 = mybir.dt.bfloat16
U32 = mybir.dt.uint32
U8 = mybir.dt.uint8
FP8X4 = mybir.dt.float8_e4m3fn_x4
ALU = mybir.AluOpType
ACT = mybir.ActivationFunctionType

P = 128
PACK = 4
ROWS = D // PACK
SQUARE = 32
GAIN = 512.0
HALF = N // 2
PAIR = 2
DY_SCALAR = 304


def tile_rows_browsoft_kernel(tc, x, w1, w2, tp, wo, dy, old, out):
    nc = tc.nc
    with ExitStack() as ctx:
        sb = ctx.enter_context(tc.tile_pool(name="sb", bufs=1))
        ps = ctx.enter_context(tc.psum_pool(name="ps", bufs=1))
        ctx.enter_context(tc.manual_schedule())

        def load(name, src, width):
            raw = sb.tile([P, PACK, width], F32, name=name)
            nc.sync.dma_start(out=raw[:], in_=src.rearrange("g (p j) c -> (g p) j c", j=PACK))
            return raw

        def operand(name, width):
            return {
                "values": sb.tile([P, width, PACK], BF16, name=name + "_bf16", align_bytes=64),
                "codes": sb.tile([P, width], U32, name=name + "_codes", align_bytes=64),
                "scales": sb.tile([P, width], U8, name=name + "_scales", align_bytes=64),
            }

        def interleave(copy, mx, at, raw, first, last, run):
            dst = mx["values"][:, at + first : at + last, :].rearrange("p (c i) j -> p c j i", i=run)
            src = raw[:, :, first:last].rearrange("p j (c i) -> p c j i", i=run)
            copy(out=dst, in_=src)

        def gpsimd_copy(out, in_):
            nc.gpsimd.tensor_scalar(out=out, in0=in_, scalar1=1.0, scalar2=0.0, op0=ALU.mult, op1=ALU.add)

        def quantize(mx, first, last):
            nc.vector.quantize_mx(
                out=mx["codes"][:, first:last].bitcast(FP8X4),
                scales=mx["scales"][:, first:last],
                in_=mx["values"][:, first:last, :].rearrange("p c j -> p (c j)"),
            )

        def product(bank, g, w_mx, at, act_mx):
            rows = slice(ROWS * g, ROWS * (g + 1))
            nc.tensor.matmul_mx(
                out=bank[:],
                lhsT=w_mx["codes"][rows, at : at + M].bitcast(FP8X4),
                lhsT_scale=w_mx["scales"][rows, at : at + M],
                rhs=act_mx["codes"][rows, :].bitcast(FP8X4),
                rhs_scale=act_mx["scales"][rows, :],
                start=True,
                stop=True,
            )

        tp_rows = sb.tile([P, P], F32, name="tp_rows", align_bytes=64)
        tp_cols = sb.tile([P, P], F32, name="tp_cols", align_bytes=64)
        nc.vector.memset(tp_rows[:], 0.0)

        x_raw = load("x_raw", x, N)
        nc.sync.dma_start(
            out=tp_rows[0:P:SQUARE, :].rearrange("a (g c) -> a g c", g=G),
            in_=tp.rearrange("g (a c) o -> a g (c o)", c=SQUARE),
        )
        w1_raw = load("w1_raw", w1, M)
        w2_raw = load("w2_raw", w2, M)
        wo_raw = load("wo_raw", wo, M)
        dy_raw = load("dy_raw", dy, N)
        old_sb = []
        for pair in range(G // 2):
            old_pair = sb.tile([P, 2, N], F32, name="old_%d" % pair)
            nc.sync.dma_start(out=old_pair[:], in_=old[2 * pair : 2 * pair + 2].rearrange("g m n -> m g n"))
            old_sb.extend([old_pair[:, 0, :], old_pair[:, 1, :]])

        neg_tp = sb.tile([P, G], F32, name="neg_tp")
        neg_gain = sb.tile([P, G], F32, name="neg_gain")

        x_mx = operand("x", N)
        dy_mx = operand("dy", N)
        w1_mx = operand("w1", M)
        w2wo_mx = operand("w2wo", 2 * M)
        bank_z1c0 = [ps.tile([M, N], F32, name="bank_z1c0_%d" % g) for g in range(G)]
        bank_z2 = [ps.tile([M, N], F32, name="bank_z2_%d" % g) for g in range(G)]

        neg_s = [sb.tile([M, N], F32, name="neg_s%d" % g) for g in range(G)]
        p1 = [sb.tile([M, N], F32, name="p1_%d" % g) for g in range(G)]
        neg_pz = [sb.tile([M, N], F32, name="neg_pz%d" % g) for g in range(G)]
        neg_u = [sb.tile([M, N], F32, name="neg_u%d" % g) for g in range(G)]
        old_u = [sb.tile([M, N], F32, name="old_u%d" % g) for g in range(G)]
        res = [sb.tile([M, N], F32, name="res%d" % g) for g in range(G)]
        neg_max = sb.tile([M, G], F32, name="neg_max")
        zs = sb.tile([M, G], F32, name="zs")
        inv_zs = sb.tile([M, G], F32, name="inv_zs")
        neg_sum = sb.tile([M, G], F32, name="neg_sum")
        shift = sb.tile([M, G], F32, name="shift")

        def col(stats, g):
            return stats[:, g : g + 1]

        def scores(g):
            nc.vector.tensor_scalar(
                out=neg_s[g][:], in0=bank_z1c0[g][:], scalar1=col(neg_tp, g), scalar2=None,
                op0=ALU.mult, op1=ALU.min, accum_out=col(neg_max, g),
            )

        def exps(g):
            nc.scalar.activation(
                out=p1[g][:], in_=neg_s[g][:], func=ACT.Exp, scale=-1.0, bias=col(neg_max, g), accum_out=col(zs, g),
            )

        def times_z2(g):
            nc.vector.scalar_tensor_tensor(
                out=neg_pz[g][:], in0=bank_z2[g][:], scalar=col(neg_gain, g), in1=p1[g][:], op0=ALU.mult, op1=ALU.mult,
            )

        def times_z2_off_vector(g):
            neg_z2 = sb.tile([M, N], F32, name="neg_z2")
            nc.scalar.activation(out=neg_z2[:], in_=bank_z2[g][:], func=ACT.Copy, scale=col(neg_gain, g))
            nc.gpsimd.tensor_tensor(out=neg_pz[g][:], in0=neg_z2[:], in1=p1[g][:], op=ALU.mult)

        def inverses(first, last):
            nc.vector.reciprocal(out=inv_zs[:, first:last], in_=zs[:, first:last])

        def times_c0(g):
            nc.vector.scalar_tensor_tensor(
                out=neg_u[g][:], in0=bank_z1c0[g][:], scalar=col(inv_zs, g), in1=neg_pz[g][:],
                op0=ALU.mult, op1=ALU.mult, accum_out=col(neg_sum, g),
            )
            nc.scalar.activation(out=col(shift, g), in_=col(neg_sum, g), func=ACT.Copy, scale=col(inv_zs, g))

        def add_old(engine, g, cols):
            engine.tensor_tensor(out=old_u[g][:, cols], in0=old_sb[g][:, cols], in1=neg_u[g][:, cols], op=ALU.subtract)

        def finish(g, cols):
            nc.vector.scalar_tensor_tensor(
                out=res[g][:, cols], in0=p1[g][:, cols], scalar=col(shift, g), in1=old_u[g][:, cols],
                op0=ALU.mult, op1=ALU.add,
            )
            nc.sync.dma_start(out=out[g, :, cols], in_=res[g][:, cols])

        whole = slice(0, N)
        halves = [slice(0, HALF), slice(HALF, N)]

        interleave(nc.vector.tensor_copy, x_mx, 0, x_raw, 0, HALF, PAIR)
        interleave(nc.scalar.copy, x_mx, 0, x_raw, HALF, N, PAIR)
        interleave(nc.vector.tensor_copy, w1_mx, 0, w1_raw, 0, M, PAIR)
        quantize(x_mx, 0, HALF)
        quantize(w1_mx, 0, M)
        quantize(x_mx, HALF, N)
        for g in range(G):
            product(bank_z1c0[g], g, w1_mx, 0, x_mx)

        interleave(nc.scalar.copy, w2wo_mx, 0, w2_raw, 0, M, PAIR)
        interleave(nc.scalar.copy, w2wo_mx, M, wo_raw, 0, M, PAIR)
        nc.vector.transpose(out=tp_cols[:], in_=tp_rows[:])
        nc.vector.tensor_scalar(out=neg_tp[:], in0=tp_cols[:, 0:P:SQUARE], scalar1=-1.0, scalar2=None, op0=ALU.mult)
        nc.vector.tensor_scalar(out=neg_gain[:], in0=tp_cols[:, 0:P:SQUARE], scalar1=-GAIN, scalar2=None, op0=ALU.mult)
        quantize(w2wo_mx, 0, 2 * M)
        for g in range(G):
            product(bank_z2[g], g, w2wo_mx, 0, x_mx)

        interleave(nc.scalar.copy, dy_mx, 0, dy_raw, 0, DY_SCALAR, PAIR)
        interleave(gpsimd_copy, dy_mx, 0, dy_raw, DY_SCALAR, N, 1)
        for g in range(G):
            scores(g)
        quantize(dy_mx, 0, N)
        for g in range(G):
            product(bank_z1c0[g], g, w2wo_mx, M, dy_mx)

        exps(0)
        exps(1)
        times_z2(0)
        times_z2_off_vector(1)
        exps(2)
        exps(3)
        inverses(0, 2)

        times_c0(0)
        add_old(nc.gpsimd, 0, whole)
        times_z2(2)
        times_c0(1)
        add_old(nc.gpsimd, 1, whole)
        inverses(2, 4)
        times_z2(3)
        times_c0(2)
        times_c0(3)

        finish(0, whole)
        add_old(nc.vector, 2, whole)
        finish(1, whole)
        finish(2, whole)
        for cols in halves:
            add_old(nc.vector, 3, cols)
        for cols in halves:
            finish(3, cols)
